import numpy as np, ml_dtypes
CORES = [18,19,22,23,26,27,30,31,98,99,102,103,106,107,110,111]
N = 16
ROOT = 11
def setup_inputs(rng):
    return {"x": rng.standard_normal((N, 128, 8), dtype=np.float32).astype(ml_dtypes.bfloat16)}
def reference(x):
    y = np.full((N, 128, N * 8), np.nan, x.dtype)
    y[ROOT] = np.concatenate(list(x), axis=1)
    return {"y": y}

SCRATCH = {
    "stage": ("dram", [128, 8], "bfloat16"),
    "land": ("sbuf", [128, 128], "bfloat16"),
}
SEMAPHORES = ["loaded", "sent", "arrived", "stored"]


def _engines(mask):
    return bin(mask).count("1")


def rank_program(g, core, T, topo):
    rank = T.rank_of(core)
    if rank is None:
        return
    root = T.cores[11]
    w = 8

    if core != root:
        mask = topo.mask(core, root)
        rid, pid, _se = topo.addr(root)
        g.sync.dma_start(T.stage[:], T.x[:]).then_inc(T.sem.loaded, 16)
        g.wait_ge(T.sem.loaded, 16)
        g.remote_dma(
            T.land[:, rank * w:(rank + 1) * w],
            T.stage[:],
            remote_sem=T.sem.arrived,
            local_sem=T.sem.sent,
            pid=pid,
            routing_id=rid,
            dma_engine_mask=mask,
        )
        g.wait_ge(T.sem.sent, _engines(mask))
        return

    total = 16
    for c in T.cores:
        if c != root:
            total += _engines(topo.mask(c, root))
    g.sync.dma_start(T.land[:, rank * w:(rank + 1) * w], T.x[:]).then_inc(T.sem.arrived, 16)
    g.sync.wait_ge(T.sem.arrived, total)
    g.sync.dma_start(T.y[:], T.land[:]).then_inc(T.sem.stored, 16)
    g.sync.wait_ge(T.sem.stored, 16)
